import numpy as np, ml_dtypes
CORES = [1,5,17,21,33,37,49,53]
N = 8
import mx_ref
BF = ml_dtypes.bfloat16
def entries(a):
    return np.ascontiguousarray(a.T).reshape(-1)
def table(e):
    return np.ascontiguousarray(np.reshape(e, (-1, 16)).T).astype(np.int32)
def cols(t, e):
    v = np.concatenate([t.reshape(128, -1, 4), np.zeros((128, 1, 4), BF)], axis=1)
    return np.ascontiguousarray(v[:, e]).reshape(128, -1)
def f(rng, *shape):
    return mx_ref.flush((rng.standard_normal(shape, dtype=np.float32) * np.exp2(rng.integers(-2, 3, shape[:-1] + (1,)))).astype(BF))
def wide(rng, *shape, cols=0):
    v = rng.standard_normal(shape, dtype=np.float32) * np.exp2(rng.integers(-12, 13, shape)).astype(np.float32)
    if cols: v *= np.repeat(np.exp2(rng.integers(-cols, cols + 1, shape[:-2] + (1, shape[-1] // 4))) * (rng.random(shape[:-2] + (1, shape[-1] // 4)) > 0.0625), 4, axis=-1).astype(np.float32)
    return mx_ref.flush(v.astype(BF))
B, K, O = 320, 96, 3
def order(r):
    return [(r + 1 + i) % N for i in range(N)]
def some(rng, where, n):
    e = np.full(K, -1); e[rng.permutation(K)[:n]] = rng.permutation(where)[:n]
    return table(e)
def setup_inputs(rng):
    return {"b": f(rng, N, 128, 4 * B), "x": f(rng, N, 128, 4 * K), "w": f(rng, N, 128, 512 * O), "pl": np.stack([some(rng, np.arange(B), int(rng.integers(K >> 1, K + 1))) for r in range(N)])}
def setup_inputs_same(rng):
    d = setup_inputs(rng)
    for i in range(50):
        at = rng.permutation(B)[:K]; quiet = rng.permutation(N)[:int(rng.integers(1, 3))].tolist()
        pl = [some(rng, at, 0 if r in quiet else int(rng.integers(K >> 2, (3 * K >> 2) + 1))) for r in range(N)]
        s = [set(entries(pl[r]).tolist()) - {-1} for r in range(N) if r not in quiet]
        if all(s[j] & s[k] for j in range(len(s)) for k in range(j)):
            d["pl"] = np.stack(pl); return d
    raise RuntimeError("no draw in which any two of the writing ranks have a place in common")
def setup_inputs_apart(rng):
    d = setup_inputs(rng); at, start = rng.permutation(B), int(rng.integers(N))
    pl = [None] * N
    for i in range(N):
        e = at[K * i:K * i + K]
        pl[(start + i) % N] = some(rng, e, len(e))
    d["pl"] = np.stack(pl); return d
def setup_inputs_runs(rng):
    d = setup_inputs(rng); p = rng.permutation(N)
    pl = [None] * N
    for i in range(N):
        if i == 0: at = np.arange(0)
        elif i % 3 == 1: at = (int(rng.integers(B)) + np.arange(K)) % B
        elif i % 3 == 2: at = np.flatnonzero(np.isin(np.arange(B) % 8, rng.permutation(8)[:8 * K // B]))
        else: at = rng.permutation(B)[:K - int(rng.integers(K >> 2, (3 * K >> 2) + 1))]
        at = rng.permutation(at); a = int(rng.integers(len(at) + 1))
        pl[p[i]] = table(np.concatenate([at[:a], np.full(K - len(at), -1), at[a:]]))
    d["pl"] = np.stack(pl); return d
def setup_inputs_halves(rng):
    d = setup_inputs(rng); at, start = rng.permutation(B), int(rng.integers(N))
    pl = [None] * N
    for i in range(N): pl[(start + i) % N] = some(rng, at[:B >> 1] if i < N >> 1 else at[B >> 1:], K)
    d["pl"] = np.stack(pl); return d
def setup_inputs_spread(rng):
    d = setup_inputs(rng); d["b"] = wide(rng, N, 128, 4 * B, cols=6); d["x"] = wide(rng, N, 128, 4 * K, cols=6); return d
def check_inputs(d):
    bad = []
    for r in range(N):
        e = entries(d["pl"][r])
        if e.min() < -1 or e.max() >= B: bad.append("pl")
        e = e[e >= 0]
        if len(set(e.tolist())) != len(e): bad.append("pl names a place twice")
    return bad
def reference(b, x, w, pl):
    y = np.zeros((N, 128, O * B), np.float32)
    for r in range(N):
        m = np.array(b[r]).reshape(128, B, 4)
        for s in order(r):
            e = entries(pl[s]); k = np.flatnonzero(e >= 0)
            m[:, e[k]] = x[s].reshape(128, K, 4)[:, k]
        q = mx_ref.quantize(m.reshape(128, 4 * B))
        for o in range(O):
            y[r][:, B * o:B * o + B] = mx_ref.matmul(mx_ref.quantize(cols(w[r], np.arange(128 * o, 128 * o + 128))), q)
    return {"y": y}

@@ -1,0 +1,244 @@
+from concourse.bass import DstId, RemoteDMATransfer
+from concourse.mybir import dt, AluOpType, ActivationFunctionType
+
+B, K, O = 320, 96, 3
+FAR, PASSED, MATE, OWN = B, B + 3 * K, B + 6 * K, B + 7 * K
+WIDE = B + 8 * K
+SLOT = 128
+HALF = B // 2
+PRIO = 2048
+
+
+def _sb(n, t):
+    return ("sbuf", [128, n], t)
+
+
+F, I, U, H, C = "float32", "int32", "uint16", "bfloat16", "float8_e4m3fn_x4"
+SCRATCH = {
+    "lo": ("dram", [SLOT, 1], I), "land": ("dram", [8, SLOT, 1], I),
+    "xt": _sb(512, H), "bt": _sb(4 * B, H), "wt": _sb(512 * O, H),
+    "qc": _sb(WIDE + 32, C), "qs": _sb(WIDE + 32, "uint8"), "wq": _sb(128 * O, C), "ws": _sb(128 * O, "uint8"),
+    "mq": _sb(B, C), "ms": _sb(B, "uint8"),
+    "idx": _sb(K, I), "six": _sb(K, I), "k16": _sb(K, F), "k95": _sb(K, F), "kk": _sb(K, F), "val": _sb(4 * K, F),
+    "part": _sb(1, I), "par": _sb(1, I), "pcol": _sb(4, F), "di": _sb(64, I), "dm": _sb(64, I), "dump": _sb(64, F),
+    "pk": _sb(64, I), "zl": _sb(64, F), "tl": _sb(64, F), "off": _sb(32, U), "bl": _sb(B, F),
+    "win": _sb(SLOT * (B + 1), F), "dup": ("sbuf", [128, 20, 32], F), "tr": ("sbuf", [128, 20, 32], F),
+    "best": _sb(20, I), "bcol": _sb(20, I), "pick": _sb(20, U), "yt": _sb(O * B, F), "ps": ("psum", [128, 512 * 6], F),
+}
+SEMAPHORES = ["lp", "ow", "sx", "sb", "sw", "gi", "gb", "wi", "v", "mz", "qx", "qb", "qw", "loc", "al", "ac", "asc", "pc",
+              "psc", "fc", "fs", "ls", "lc", "sc", "sd", "of", "pa", "pb", "sa", "sb2", "m0", "m1", "m2", "m3", "m4", "m5",
+              "y0", "y1", "y2", "st"]
+
+
+def rank_program(g, core, T, topo):
+    rank = T.rank_of(core)
+    if rank is None:
+        return
+    cores, S = T.cores, T.sem
+    n = len(cores)
+    ADD, MUL, MAX, SUB, AND = AluOpType.add, AluOpType.mult, AluOpType.max, AluOpType.subtract, AluOpType.bitwise_and
+    COPY = ActivationFunctionType.Copy
+
+    def order(r):
+        return [(r + 1 + i) % n for i in range(n)]
+
+    def same_chip(a, b):
+        return topo.chip(cores[a]) == topo.chip(cores[b])
+
+    def far(r):
+        return [s for s in order(r)[:-1] if not same_chip(r, s) and topo.die(cores[s]) == topo.die(cores[r])]
+
+    def partner(r):
+        return [s for s in order(r)[:-1] if same_chip(r, s)][0]
+
+    def dst(r):
+        rid, pid, _ = topo.addr(cores[r])
+        return DstId(rid=rid, pnc=pid)
+
+    mate = partner(rank)
+    faraway = far(rank)
+    base = {rank: OWN, mate: MATE}
+    for d, s in enumerate(faraway):
+        base[s] = FAR + K * d
+    for d, s in enumerate(far(mate)):
+        base[s] = PASSED + K * d
+
+    eoff = topo.engines(core, cores[faraway[0]])
+    eall = topo.engines(core, cores[mate])
+    eon = [e for e in eall if e not in eoff]
+    moff = topo.mask(core, cores[faraway[0]])
+    mon = sum(1 << e for e in eon)
+    mall = topo.mask(core, cores[mate])
+
+    sy, sl = g.sync, g.scalar
+    sy.dma_start(T.lo[0:K, :], T.pl[:, :]).then_inc(S.lp, 16)
+    sy.dma_start(T.lo[K:SLOT, :], T.pl[0:16, 0:2]).then_inc(S.lp, 16)
+    sl.dma_start(T.xt[:, 0:4 * K], T.x[:, :]).then_inc(S.sx, 16)
+    sl.dma_start(T.bt[:, :], T.b[:, :]).then_inc(S.sb, 16)
+    sy.dma_start(T.wt[:, :], T.w[:, :]).then_inc(S.sw, 16)
+
+    g.iota(T.idx[:, :], [[32, 3], [1, 2], [2, 16]], 0, 0).then_inc(S.gi, 1)
+    g.iota(T.di[:, :], [[0, 2], [1, 32]], 0, 32).then_inc(S.gi, 1)
+    g.iota(T.part[:, :], [[1, 1]], 0, 1).then_inc(S.gi, 1)
+    others = [s for s in order(rank)[:-1] if s != mate]
+    half = len(others) // 2
+    g.wait_ge(S.lp, 32)
+
+    def slot_at(r):
+        return T.land[order(r).index(rank)]
+
+    g.remote_dma_fused([
+        RemoteDMATransfer(dst_ids=[dst(s) for s in to], dma_engine_mask=1 << e, remote_sem=S.al,
+                          srcs=[T.lo[:, :]], dsts=[slot_at(s) for s in to])
+        for e, to in ((eoff[0], others[:half]), (eoff[len(eoff) // 2], others[half:] + [mate]))], local_sem=S.loc)
+    loc = 2
+    n_lists = n - 1
+
+    def at(r):
+        return FAR + K * far(r).index(rank)
+
+    g.wait_ge(S.qx, 1)
+    for codes in (True, False):
+        def view(a, m):
+            return T.qc[:, a:a + m].bitcast(dt.uint8) if codes else T.qs[:, a:a + m]
+        g.remote_dma_fused([
+            RemoteDMATransfer(dst_ids=[dst(s) for s in faraway], dma_engine_mask=moff, remote_sem=S.ac if codes else S.asc,
+                              srcs=[view(OWN, K)], dsts=[view(at(s), K) for s in faraway]),
+            RemoteDMATransfer(dst_ids=[dst(mate)], dma_engine_mask=mon, remote_sem=S.pc if codes else S.psc,
+                              srcs=[view(OWN, K)], dsts=[view(MATE, K)]),
+        ], local_sem=S.loc)
+        loc += len(eoff) + len(eon)
+    n_far, n_mate = len(faraway) * len(eoff), len(eon)
+    g.iota(T.bl[:, :], [[1, B]], 0, 0, allow_small_or_imprecise_dtypes=True).then_inc(S.gb, 1)
+    rid, pid, _ = topo.addr(cores[mate])
+    g.wait_ge(S.ac, n_far)
+    g.remote_dma(T.qc[:, PASSED:PASSED + 3 * K].bitcast(dt.uint8), T.qc[:, FAR:FAR + 3 * K].bitcast(dt.uint8),
+                 S.fc, S.loc, pid, rid, mon)
+    g.wait_ge(S.asc, n_far)
+    g.remote_dma(T.qs[:, PASSED:PASSED + 3 * K], T.qs[:, FAR:FAR + 3 * K], S.fs, S.loc, pid, rid, mall)
+    loc += len(eon) + len(eall)
+    g.wait_ge(S.loc, loc)
+
+    places = T.win[:, SLOT:SLOT * (B + 1):SLOT]
+    sy.wait_ge(S.lp, 32)
+    sy.dma_start(T.land[n - 1], T.lo[:, :]).then_inc(S.ow, 16)
+    for q, sem, blocks in ((sy, S.ls, (0, 1)), (sl, S.lc, (2, 3))):
+        q.wait_ge(S.mz, 1)
+        q.wait_ge(S.ow, 16)
+        q.wait_ge(S.al, n_lists)
+        for k in blocks:
+            for u in (0, 1):
+                q.dma_start(T.pk[32 * k:32 * k + 16, 32 * u:32 * u + 32], T.land[4 * u:4 * u + 4]).then_inc(sem, 16)
+
+    ve, cnt = g.vector, [0]
+
+    def did(ins):
+        ins.then_inc(S.v, 1)
+        cnt[0] += 1
+
+    def settle():
+        ve.wait_ge(S.v, cnt[0])
+
+    did(ve.memset(T.xt[:, 4 * K:512], 0.0))
+    ve.memset(T.pk[:, :], 0).then_inc(S.mz, 1)
+    ve.wait_ge(S.sx, 16)
+    settle()
+    ve.quantize_mx(T.qc[:, OWN:OWN + 128], T.qs[:, OWN:OWN + 128], T.xt[:, :]).then_inc(S.qx, 1)
+    ve.wait_ge(S.gi, 3)
+    did(ve.tensor_scalar(T.six[:, :], T.idx[:, :], 1.0 / 6.0, -2.5 / 6.0, MUL, ADD))
+    did(ve.tensor_scalar(T.k16[:, :], T.idx[:, :], 16.0, None, MUL))
+    did(ve.tensor_scalar(T.par[:, :], T.part[:, :], 16, None, AND))
+    did(ve.tensor_scalar(T.dm[:, :], T.di[:, :], SLOT - 1, None, AND))
+    settle()
+    did(ve.tensor_scalar(T.k95[:, :], T.six[:, :], 95.0, None, MUL))
+    did(ve.tensor_scalar(T.dump[:, :], T.dm[:, :], -1.0 / SLOT, -1.0 / SLOT, MUL, ADD))
+    o = order(rank)
+    first = [[PRIO * (4 * u + t + 1) + base[o[4 * u + t]] for u in (0, 1)] for t in range(4)]
+    for t in range(4):
+        did(ve.tensor_scalar(T.pcol[:, t:t + 1], T.par[:, :], (first[t][1] - first[t][0]) / 16.0, float(first[t][0]), MUL, ADD))
+    settle()
+    did(ve.tensor_tensor(T.kk[:, :], T.k16[:, :], T.k95[:, :], SUB))
+    settle()
+    for t in range(4):
+        did(ve.tensor_scalar(T.val[:, K * t:K * t + K], T.kk[:, :], T.pcol[:, t:t + 1], None, ADD))
+    ve.wait_ge(S.sb, 16)
+    ve.quantize_mx(T.qc[:, 0:B], T.qs[:, 0:B], T.bt[:, :]).then_inc(S.qb, 1)
+    ve.wait_ge(S.gb, 1)
+    ve.tensor_copy(places, T.bl[:, :]).then_inc(S.wi, 1)
+    ve.wait_ge(S.sw, 16)
+    ve.quantize_mx(T.wq[:, :], T.ws[:, :], T.wt[:, :]).then_inc(S.qw, 1)
+    ve.wait_ge(S.mz, 1)
+    ve.wait_ge(S.wi, 1)
+    settle()
+    ve.wait_ge(S.ls, 64)
+    ve.wait_ge(S.lc, 64)
+    for X in (0, 1):
+        did(ve.tensor_tensor(T.zl[:, 32 * X:32 * X + 32], T.pk[:, X:64:2], T.dump[:, X:64:2], MAX))
+    settle()
+    did(ve.transpose(T.tl[:, :], T.zl[:, :]))
+    settle()
+    for X in (0, 1):
+        did(ve.tensor_scalar(T.off[:, X:32:2], T.tl[:, 32 * X:32 * X + 16], float(SLOT), float(SLOT), MUL, ADD))
+    for t in range(4):
+        settle()
+        ins = ve.tensor_copy(T.win[:, :].indirect(T.off[:, 8 * t:8 * t + 6]), T.val[:, K * t:K * t + K])
+        if t < 3:
+            did(ins)
+        else:
+            ins.then_inc(S.sc, 1)
+    ve.wait_ge(S.sc, 1)
+    did(ve.tensor_copy(T.dup[:, :, 0:16], places))
+    settle()
+    ve.wait_ge(S.sd, 1)
+    did(ve.transpose(T.tr[:, :, :], T.dup[:, :, :]))
+    settle()
+    did(ve.tensor_tensor(T.best[:, :], T.tr[:, :, 0], T.tr[:, :, 16], MAX))
+    settle()
+    did(ve.tensor_scalar(T.bcol[:, :], T.best[:, :], PRIO - 1, None, AND))
+    settle()
+    ve.tensor_copy(T.pick[:, :], T.bcol[:, :]).then_inc(S.of, 1)
+    ve.wait_ge(S.of, 1)
+    ve.wait_ge(S.qx, 1)
+    ve.wait_ge(S.qb, 1)
+    ve.wait_ge(S.pc, n_mate)
+    ve.wait_ge(S.ac, n_far)
+    ve.wait_ge(S.fc, len(eon))
+    for h, sem in ((0, S.pa), (1, S.pb)):
+        ve.tensor_copy(T.mq[:, HALF * h:HALF * h + HALF].bitcast(dt.uint32),
+                       T.qc[:, 0:WIDE].bitcast(dt.uint32).indirect(T.pick[:, 10 * h:10 * h + 10])).then_inc(sem, 1)
+
+    sl.wait_ge(S.sc, 1)
+    sl.activation(T.dup[:, :, 16:32], places, COPY).then_inc(S.sd, 1)
+    sl.wait_ge(S.qx, 1)
+    sl.wait_ge(S.qb, 1)
+    sl.wait_ge(S.of, 1)
+    sl.wait_ge(S.psc, n_mate)
+    sl.wait_ge(S.asc, n_far)
+    sl.wait_ge(S.fs, len(eall))
+    for h, sem in ((0, S.sa), (1, S.sb2)):
+        sl.activation(T.ms[:, HALF * h:HALF * h + HALF], T.qs[:, 0:WIDE].indirect(T.pick[:, 10 * h:10 * h + 10]), COPY).then_inc(sem, 1)
+
+    te = g.tensor
+    runs = [(0, 0), (1, 0), (0, 1), (1, 1), (2, 0), (2, 1)]
+    te.wait_ge(S.qw, 1)
+    waited = []
+    for i, (r, h) in enumerate(runs):
+        if h not in waited:
+            te.wait_ge((S.pa, S.pb)[h], 1)
+            te.wait_ge((S.sa, S.sb2)[h], 1)
+            waited.append(h)
+        te.matmul_mx(T.ps[:, 512 * i:512 * i + HALF], T.wq[:, 128 * r:128 * r + 128], T.ws[:, 128 * r:128 * r + 128],
+                     T.mq[:, HALF * h:HALF * h + HALF], T.ms[:, HALF * h:HALF * h + HALF], True, True).then_inc(S["m%d" % i], 1)
+    for i, (r, h) in enumerate(runs):
+        out = T.yt[:, B * r + HALF * h:B * r + HALF * h + HALF]
+        src = T.ps[:, 512 * i:512 * i + HALF]
+        if (r, h) in ((0, 0), (0, 1), (2, 1)):
+            ve.wait_ge(S["m%d" % i], 1)
+            ve.tensor_copy(out, src).then_inc(S["y%d" % r], 1)
+        else:
+            sl.wait_ge(S["m%d" % i], 1)
+            sl.activation(out, src, COPY).then_inc(S["y%d" % r], 1)
+    for r in range(O):
+        sy.wait_ge(S["y%d" % r], 2)
+        sy.dma_start(T.y[:, B * r:B * r + B], T.yt[:, B * r:B * r + B]).then_inc(S.st, 16)
+    sy.wait_ge(S.st, 48)

@@ -2,11 +2,13 @@ from concourse.bass import DstId, RemoteDMATransfer
 from concourse.mybir import dt, AluOpType, ActivationFunctionType
 
 B, K, O = 320, 96, 3
-FAR, PASSED, MATE, OWN = B, B + 3 * K, B + 6 * K, B + 7 * K
+G = 16
 WIDE = B + 8 * K
+OWN = WIDE - K
 SLOT = 128
 HALF = B // 2
 PRIO = 2048
+KEEP, DROP = 16 * PRIO, -64 * PRIO
 
 
 def _sb(n, t):
@@ -15,18 +17,18 @@ def _sb(n, t):
 
 F, I, U, H, C = "float32", "int32", "uint16", "bfloat16", "float8_e4m3fn_x4"
 SCRATCH = {
-    "lo": ("dram", [SLOT, 1], I), "land": ("dram", [8, SLOT, 1], I),
+    "lo": ("dram", [SLOT, 1], I), "land": ("dram", [7, SLOT, 1], I),
     "xt": _sb(512, H), "bt": _sb(4 * B, H), "wt": _sb(512 * O, H),
     "qc": _sb(WIDE + 32, C), "qs": _sb(WIDE + 32, "uint8"), "wq": _sb(128 * O, C), "ws": _sb(128 * O, "uint8"),
     "mq": _sb(B, C), "ms": _sb(B, "uint8"),
-    "idx": _sb(K, I), "six": _sb(K, I), "k16": _sb(K, F), "k95": _sb(K, F), "kk": _sb(K, F), "val": _sb(4 * K, F),
-    "part": _sb(1, I), "par": _sb(1, I), "pcol": _sb(4, F), "di": _sb(64, I), "dm": _sb(64, I), "dump": _sb(64, F),
-    "pk": _sb(64, I), "zl": _sb(64, F), "tl": _sb(64, F), "off": _sb(32, U), "bl": _sb(B, F),
-    "win": _sb(SLOT * (B + 1), F), "dup": ("sbuf", [128, 20, 32], F), "tr": ("sbuf", [128, 20, 32], F),
+    "ones": _sb(B, H), "diag": _sb(G, I), "dm": _sb(G, I), "blk": _sb(1, I), "odd": _sb(1, I), "cb": _sb(1, F), "ch": _sb(1, F),
+    "na": _sb(1, F), "e0": _sb(G, F), "e1": _sb(G, F), "gate": _sb(B, F), "val": _sb(K, F), "dump": _sb(6, F),
+    "pk": _sb(8, I), "zl": _sb(6, F), "off": _sb(6, U), "win": _sb(SLOT * (B + 1), F), "run": _sb(512, F),
+    "t1": _sb(32, F), "t2": _sb(32, F), "t3": _sb(64, F), "t4": _sb(40, F),
     "best": _sb(20, I), "bcol": _sb(20, I), "pick": _sb(20, U), "yt": _sb(O * B, F), "ps": ("psum", [128, 512 * 6], F),
 }
-SEMAPHORES = ["lp", "ow", "sx", "sb", "sw", "gi", "gb", "wi", "v", "mz", "qx", "qb", "qw", "loc", "al", "ac", "asc", "pc",
-              "psc", "fc", "fs", "ls", "lc", "sc", "sd", "of", "pa", "pb", "sa", "sb2", "m0", "m1", "m2", "m3", "m4", "m5",
+SEMAPHORES = ["lp", "sx", "sb", "sw", "gi", "v", "a", "g16", "qx", "qb", "qw", "loc", "al", "ac", "asc", "pc",
+              "psc", "fc", "fs", "ls", "li", "of", "pa", "pb", "sa", "sb2", "m0", "m1", "m2", "m3", "m4", "m5",
               "y0", "y1", "y2", "st"]
 
 
@@ -36,7 +38,8 @@ def rank_program(g, core, T, topo):
         return
     cores, S = T.cores, T.sem
     n = len(cores)
-    ADD, MUL, MAX, SUB, AND = AluOpType.add, AluOpType.mult, AluOpType.max, AluOpType.subtract, AluOpType.bitwise_and
+    ADD, MUL, MAX, AND = AluOpType.add, AluOpType.mult, AluOpType.max, AluOpType.bitwise_and
+    SHR, EQ = AluOpType.arith_shift_right, AluOpType.is_equal
     COPY = ActivationFunctionType.Copy
 
     def order(r):
@@ -55,13 +58,15 @@ def rank_program(g, core, T, topo):
         rid, pid, _ = topo.addr(cores[r])
         return DstId(rid=rid, pnc=pid)
 
+    def col(r, s):
+        slot = order(r).index(s)
+        return B + 4 * K * (slot % 2) + K * (slot // 2)
+
     mate = partner(rank)
     faraway = far(rank)
-    base = {rank: OWN, mate: MATE}
-    for d, s in enumerate(faraway):
-        base[s] = FAR + K * d
-    for d, s in enumerate(far(mate)):
-        base[s] = PASSED + K * d
+    FAR, PASSED, MATE = col(rank, faraway[0]), col(mate, faraway[0]), col(mate, rank)
+    assert [col(rank, s) for s in faraway] == [FAR + K * i for i in range(3)]
+    assert [col(mate, s) for s in faraway] == [PASSED + K * i for i in range(3)]
 
     eoff = topo.engines(core, cores[faraway[0]])
     eall = topo.engines(core, cores[mate])
@@ -76,10 +81,9 @@ def rank_program(g, core, T, topo):
     sl.dma_start(T.xt[:, 0:4 * K], T.x[:, :]).then_inc(S.sx, 16)
     sl.dma_start(T.bt[:, :], T.b[:, :]).then_inc(S.sb, 16)
     sy.dma_start(T.wt[:, :], T.w[:, :]).then_inc(S.sw, 16)
+    sy.dma_start(T.pk[G * (n - 1):G * n, 0:6], T.pl[:, :]).then_inc(S.ls, 16)
 
-    g.iota(T.idx[:, :], [[32, 3], [1, 2], [2, 16]], 0, 0).then_inc(S.gi, 1)
-    g.iota(T.di[:, :], [[0, 2], [1, 32]], 0, 32).then_inc(S.gi, 1)
-    g.iota(T.part[:, :], [[1, 1]], 0, 1).then_inc(S.gi, 1)
+    g.iota(T.diag[:, :], [[-1, G]], 128, 1).then_inc(S.gi, 1)
     others = [s for s in order(rank)[:-1] if s != mate]
     half = len(others) // 2
     g.wait_ge(S.lp, 32)
@@ -94,41 +98,39 @@ def rank_program(g, core, T, topo):
     loc = 2
     n_lists = n - 1
 
-    def at(r):
-        return FAR + K * far(r).index(rank)
+    def codes(a, m):
+        return T.qc[:, a:a + m].bitcast(dt.uint8)
+
+    def scales(a, m):
+        return T.qs[:, a:a + m]
+
+    def to_far(view, sem):
+        return RemoteDMATransfer(dst_ids=[dst(s) for s in faraway], dma_engine_mask=moff, remote_sem=sem,
+                                 srcs=[view(OWN, K)], dsts=[view(col(s, rank), K) for s in faraway])
+
+    def to_mate(view, sem):
+        return RemoteDMATransfer(dst_ids=[dst(mate)], dma_engine_mask=mon, remote_sem=sem,
+                                 srcs=[view(OWN, K)], dsts=[view(MATE, K)])
 
     g.wait_ge(S.qx, 1)
-    for codes in (True, False):
-        def view(a, m):
-            return T.qc[:, a:a + m].bitcast(dt.uint8) if codes else T.qs[:, a:a + m]
-        g.remote_dma_fused([
-            RemoteDMATransfer(dst_ids=[dst(s) for s in faraway], dma_engine_mask=moff, remote_sem=S.ac if codes else S.asc,
-                              srcs=[view(OWN, K)], dsts=[view(at(s), K) for s in faraway]),
-            RemoteDMATransfer(dst_ids=[dst(mate)], dma_engine_mask=mon, remote_sem=S.pc if codes else S.psc,
-                              srcs=[view(OWN, K)], dsts=[view(MATE, K)]),
-        ], local_sem=S.loc)
-        loc += len(eoff) + len(eon)
+    g.remote_dma_fused([to_far(codes, S.ac)], local_sem=S.loc)
+    g.remote_dma_fused([to_mate(codes, S.pc)], local_sem=S.loc)
+    g.wait_ge(S.li, 1)
+    g.remote_dma_fused([to_far(scales, S.asc), to_mate(scales, S.psc)], local_sem=S.loc)
+    loc += 2 * (len(eoff) + len(eon))
     n_far, n_mate = len(faraway) * len(eoff), len(eon)
-    g.iota(T.bl[:, :], [[1, B]], 0, 0, allow_small_or_imprecise_dtypes=True).then_inc(S.gb, 1)
     rid, pid, _ = topo.addr(cores[mate])
     g.wait_ge(S.ac, n_far)
-    g.remote_dma(T.qc[:, PASSED:PASSED + 3 * K].bitcast(dt.uint8), T.qc[:, FAR:FAR + 3 * K].bitcast(dt.uint8),
-                 S.fc, S.loc, pid, rid, mon)
+    g.remote_dma(codes(PASSED, 3 * K), codes(FAR, 3 * K), S.fc, S.loc, pid, rid, mon)
     g.wait_ge(S.asc, n_far)
-    g.remote_dma(T.qs[:, PASSED:PASSED + 3 * K], T.qs[:, FAR:FAR + 3 * K], S.fs, S.loc, pid, rid, mall)
+    g.remote_dma(scales(PASSED, 3 * K), scales(FAR, 3 * K), S.fs, S.loc, pid, rid, mall)
     loc += len(eon) + len(eall)
     g.wait_ge(S.loc, loc)
 
     places = T.win[:, SLOT:SLOT * (B + 1):SLOT]
-    sy.wait_ge(S.lp, 32)
-    sy.dma_start(T.land[n - 1], T.lo[:, :]).then_inc(S.ow, 16)
-    for q, sem, blocks in ((sy, S.ls, (0, 1)), (sl, S.lc, (2, 3))):
-        q.wait_ge(S.mz, 1)
-        q.wait_ge(S.ow, 16)
-        q.wait_ge(S.al, n_lists)
-        for k in blocks:
-            for u in (0, 1):
-                q.dma_start(T.pk[32 * k:32 * k + 16, 32 * u:32 * u + 32], T.land[4 * u:4 * u + 4]).then_inc(sem, 16)
+    sy.wait_ge(S.al, n_lists)
+    sy.dma_start(T.pk[0:G * n_lists, 0:6], T.land[0:n_lists, 0:K, :]).then_inc(S.ls, 16)
+    sy.sem_inc(S.li, 1)
 
     ve, cnt = g.vector, [0]
 
@@ -140,61 +142,64 @@ def rank_program(g, core, T, topo):
         ve.wait_ge(S.v, cnt[0])
 
     did(ve.memset(T.xt[:, 4 * K:512], 0.0))
-    ve.memset(T.pk[:, :], 0).then_inc(S.mz, 1)
+    did(ve.memset(T.ones[:, :], 1.0))
+    did(ve.memset(T.run[:, B:512], 0.0))
+    settle()
+    did(ve.tensor_tensor_scan(places, T.ones[:, :], T.ones[:, :], -1.0, ADD, MUL))
     ve.wait_ge(S.sx, 16)
-    settle()
     ve.quantize_mx(T.qc[:, OWN:OWN + 128], T.qs[:, OWN:OWN + 128], T.xt[:, :]).then_inc(S.qx, 1)
-    ve.wait_ge(S.gi, 3)
-    did(ve.tensor_scalar(T.six[:, :], T.idx[:, :], 1.0 / 6.0, -2.5 / 6.0, MUL, ADD))
-    did(ve.tensor_scalar(T.k16[:, :], T.idx[:, :], 16.0, None, MUL))
-    did(ve.tensor_scalar(T.par[:, :], T.part[:, :], 16, None, AND))
-    did(ve.tensor_scalar(T.dm[:, :], T.di[:, :], SLOT - 1, None, AND))
+    ve.wait_ge(S.gi, 1)
+    did(ve.tensor_scalar(T.dm[:, :], T.diag[:, :], G - 1, None, AND))
+    did(ve.tensor_scalar(T.blk[:, :], T.diag[:, 0:1], 5, 3, SHR, AND))
+    did(ve.tensor_scalar(T.odd[:, :], T.diag[:, 0:1], G, None, AND))
     settle()
-    did(ve.tensor_scalar(T.k95[:, :], T.six[:, :], 95.0, None, MUL))
-    did(ve.tensor_scalar(T.dump[:, :], T.dm[:, :], -1.0 / SLOT, -1.0 / SLOT, MUL, ADD))
-    o = order(rank)
-    first = [[PRIO * (4 * u + t + 1) + base[o[4 * u + t]] for u in (0, 1)] for t in range(4)]
-    for t in range(4):
-        did(ve.tensor_scalar(T.pcol[:, t:t + 1], T.par[:, :], (first[t][1] - first[t][0]) / 16.0, float(first[t][0]), MUL, ADD))
+    did(ve.tensor_scalar(T.e0[:, :], T.dm[:, :], 0.0, float(DROP), EQ, MUL))
+    did(ve.tensor_scalar(T.e1[:, :], T.dm[:, :], G - 1.0, float(KEEP), EQ, MUL))
+    did(ve.tensor_scalar(T.cb[:, :], T.blk[:, :], 2.0 * PRIO + K, float(PRIO + B), MUL, ADD))
+    did(ve.tensor_scalar(T.ch[:, :], T.odd[:, :], (PRIO + 4.0 * K) / G, None, MUL))
+    did(ve.tensor_scalar(T.na[:, :], T.dm[:, 0:1], -1.0 / SLOT, -1.0 / SLOT, MUL, ADD))
     settle()
-    did(ve.tensor_tensor(T.kk[:, :], T.k16[:, :], T.k95[:, :], SUB))
-    settle()
-    for t in range(4):
-        did(ve.tensor_scalar(T.val[:, K * t:K * t + K], T.kk[:, :], T.pcol[:, t:t + 1], None, ADD))
+    ve.tensor_tensor(T.gate[:, 0:G], T.e0[:, :], T.e1[:, :], ADD).then_inc(S.g16, 1)
+    did(ve.tensor_scalar(T.val[:, :], T.win[:, SLOT:SLOT * (K + 1):SLOT], T.cb[:, :], T.ch[:, :], ADD, ADD))
+    did(ve.tensor_scalar(T.dump[:, :], T.win[:, SLOT:SLOT * (K + 1):SLOT * G], -1.0 / SLOT, T.na[:, :], MUL, ADD))
     ve.wait_ge(S.sb, 16)
     ve.quantize_mx(T.qc[:, 0:B], T.qs[:, 0:B], T.bt[:, :]).then_inc(S.qb, 1)
-    ve.wait_ge(S.gb, 1)
-    ve.tensor_copy(places, T.bl[:, :]).then_inc(S.wi, 1)
     ve.wait_ge(S.sw, 16)
     ve.quantize_mx(T.wq[:, :], T.ws[:, :], T.wt[:, :]).then_inc(S.qw, 1)
-    ve.wait_ge(S.mz, 1)
-    ve.wait_ge(S.wi, 1)
+    sl.wait_ge(S.g16, 1)
+    have, steps = G, 0
+    while have < B:
+        m = min(have, B - have)
+        sl.activation(T.gate[:, have:have + m], T.gate[:, 0:m], COPY).then_inc(S.a, 1)
+        have, steps = have + m, steps + 1
+        sl.wait_ge(S.a, steps)
     settle()
-    ve.wait_ge(S.ls, 64)
-    ve.wait_ge(S.lc, 64)
-    for X in (0, 1):
-        did(ve.tensor_tensor(T.zl[:, 32 * X:32 * X + 32], T.pk[:, X:64:2], T.dump[:, X:64:2], MAX))
+    ve.wait_ge(S.a, steps)
+    ve.wait_ge(S.ls, 32)
+    did(ve.tensor_tensor(T.zl[:, :], T.pk[:, 0:6], T.dump[:, :], MAX))
     settle()
-    did(ve.transpose(T.tl[:, :], T.zl[:, :]))
+    did(ve.tensor_scalar(T.off[:, :], T.zl[:, :], float(SLOT), float(SLOT), MUL, ADD))
     settle()
-    for X in (0, 1):
-        did(ve.tensor_scalar(T.off[:, X:32:2], T.tl[:, 32 * X:32 * X + 16], float(SLOT), float(SLOT), MUL, ADD))
-    for t in range(4):
-        settle()
-        ins = ve.tensor_copy(T.win[:, :].indirect(T.off[:, 8 * t:8 * t + 6]), T.val[:, K * t:K * t + K])
-        if t < 3:
-            did(ins)
-        else:
-            ins.then_inc(S.sc, 1)
-    ve.wait_ge(S.sc, 1)
-    did(ve.tensor_copy(T.dup[:, :, 0:16], places))
+    did(ve.tensor_copy(T.win[:, :].indirect(T.off[:, :]), T.val[:, :]))
     settle()
-    ve.wait_ge(S.sd, 1)
-    did(ve.transpose(T.tr[:, :, :], T.dup[:, :, :]))
+    did(ve.tensor_tensor_scan(T.run[:, 0:B], T.gate[:, :], places, 0.0, ADD, MAX))
     settle()
-    did(ve.tensor_tensor(T.best[:, :], T.tr[:, :, 0], T.tr[:, :, 16], MAX))
+    did(ve.transpose(T.t1[:, :], T.run[:, G - 1:512:G]))
     settle()
-    did(ve.tensor_scalar(T.bcol[:, :], T.best[:, :], PRIO - 1, None, AND))
+    for h in (0, 1):
+        did(ve.tensor_tensor(T.t2[:, G * h:G * h + G], T.t1[:, 0:G], T.t1[:, G:2 * G], MAX))
+    settle()
+    for h in (0, 1):
+        did(ve.transpose(T.t3[0:64, 32 * h:32 * h + 32], T.t2[64 * h:64 * h + 64, :]))
+    settle()
+    for h in (0, 1):
+        did(ve.tensor_tensor(T.t4[0:32, 20 * h:20 * h + 20], T.t3[32 * h:32 * h + 32, 0:20], T.t3[32 * h:32 * h + 32, 32:52], MAX))
+    settle()
+    for h in (0, 1):
+        did(ve.tensor_tensor(T.best[32 * h:32 * h + 32, :], T.t4[0:32, 0:20], T.t4[0:32, 20:40], MAX))
+    settle()
+    for h in (0, 1):
+        did(ve.tensor_scalar(T.bcol[64 * h:64 * h + 64, :], T.best[0:64, :], PRIO - 1, None, AND))
     settle()
     ve.tensor_copy(T.pick[:, :], T.bcol[:, :]).then_inc(S.of, 1)
     ve.wait_ge(S.of, 1)
@@ -207,8 +212,6 @@ def rank_program(g, core, T, topo):
         ve.tensor_copy(T.mq[:, HALF * h:HALF * h + HALF].bitcast(dt.uint32),
                        T.qc[:, 0:WIDE].bitcast(dt.uint32).indirect(T.pick[:, 10 * h:10 * h + 10])).then_inc(sem, 1)
 
-    sl.wait_ge(S.sc, 1)
-    sl.activation(T.dup[:, :, 16:32], places, COPY).then_inc(S.sd, 1)
     sl.wait_ge(S.qx, 1)
     sl.wait_ge(S.qb, 1)
     sl.wait_ge(S.of, 1)

@@ -3,12 +3,11 @@ from concourse.mybir import dt, AluOpType, ActivationFunctionType
 
 B, K, O = 320, 96, 3
 G = 16
-WIDE = B + 8 * K
-OWN = WIDE - K
+PAD = 128 - K
+WIDE = B + 8 * K + PAD
 SLOT = 128
 HALF = B // 2
-PRIO = 2048
-KEEP, DROP = 16 * PRIO, -64 * PRIO
+KEEP, DROP = 2048.0, -8192.0
 
 
 def _sb(n, t):
@@ -17,18 +16,18 @@ def _sb(n, t):
 
 F, I, U, H, C = "float32", "int32", "uint16", "bfloat16", "float8_e4m3fn_x4"
 SCRATCH = {
-    "lo": ("dram", [SLOT, 1], I), "land": ("dram", [7, SLOT, 1], I),
+    "lo": ("dram", [K + 36, 1], I), "land": ("dram", [7, SLOT, 1], I),
     "xt": _sb(512, H), "bt": _sb(4 * B, H), "wt": _sb(512 * O, H),
-    "qc": _sb(WIDE + 32, C), "qs": _sb(WIDE + 32, "uint8"), "wq": _sb(128 * O, C), "ws": _sb(128 * O, "uint8"),
+    "qc": _sb(WIDE, C), "qs": _sb(WIDE + K, "uint8"), "wq": _sb(128 * O, C), "ws": _sb(128 * O, "uint8"),
     "mq": _sb(B, C), "ms": _sb(B, "uint8"),
-    "ones": _sb(B, H), "diag": _sb(G, I), "dm": _sb(G, I), "blk": _sb(1, I), "odd": _sb(1, I), "cb": _sb(1, F), "ch": _sb(1, F),
+    "ones": _sb(B, H), "diag": _sb(G, I), "dm": _sb(G, I), "grp": _sb(1, I), "cb": _sb(1, F), "ch": _sb(1, F),
     "na": _sb(1, F), "e0": _sb(G, F), "e1": _sb(G, F), "gate": _sb(B, F), "val": _sb(K, F), "dump": _sb(6, F),
     "pk": _sb(8, I), "zl": _sb(6, F), "off": _sb(6, U), "win": _sb(SLOT * (B + 1), F), "run": _sb(512, F),
     "t1": _sb(32, F), "t2": _sb(32, F), "t3": _sb(64, F), "t4": _sb(40, F),
-    "best": _sb(20, I), "bcol": _sb(20, I), "pick": _sb(20, U), "yt": _sb(O * B, F), "ps": ("psum", [128, 512 * 6], F),
+    "best": _sb(20, F), "pick": _sb(20, U), "yt": _sb(O * B, F), "ps": ("psum", [128, 512 * 6], F),
 }
-SEMAPHORES = ["lp", "sx", "sb", "sw", "gi", "v", "a", "g16", "qx", "qb", "qw", "loc", "al", "ac", "asc", "pc",
-              "psc", "fc", "fs", "ls", "li", "of", "pa", "pb", "sa", "sb2", "m0", "m1", "m2", "m3", "m4", "m5",
+SEMAPHORES = ["lp", "sx", "sb", "sw", "gi", "v", "a", "g16", "qx", "qb", "qw", "loc", "al", "ac0", "ac1", "ac2", "asc", "pc",
+              "psc", "fc", "ls", "li", "of", "pa", "pb", "sa", "sb2", "m0", "m1", "m2", "m3", "m4", "m5",
               "y0", "y1", "y2", "st"]
 
 
@@ -39,7 +38,7 @@ def rank_program(g, core, T, topo):
     cores, S = T.cores, T.sem
     n = len(cores)
     ADD, MUL, MAX, AND = AluOpType.add, AluOpType.mult, AluOpType.max, AluOpType.bitwise_and
-    SHR, EQ = AluOpType.arith_shift_right, AluOpType.is_equal
+    SHR, EQ, GE = AluOpType.arith_shift_right, AluOpType.is_equal, AluOpType.is_ge
     COPY = ActivationFunctionType.Copy
 
     def order(r):
@@ -58,30 +57,36 @@ def rank_program(g, core, T, topo):
         rid, pid, _ = topo.addr(cores[r])
         return DstId(rid=rid, pnc=pid)
 
+    def leads(r):
+        return order(r)[0] == partner(r)
+
     def col(r, s):
-        slot = order(r).index(s)
-        return B + 4 * K * (slot % 2) + K * (slot // 2)
+        return B + K * order(r).index(s) + (PAD if s == r and leads(r) else 0)
+
+    def beside(r):
+        return col(r, r) + K if leads(r) else col(r, partner(r))
 
     mate = partner(rank)
     faraway = far(rank)
-    FAR, PASSED, MATE = col(rank, faraway[0]), col(mate, faraway[0]), col(mate, rank)
-    assert [col(rank, s) for s in faraway] == [FAR + K * i for i in range(3)]
-    assert [col(mate, s) for s in faraway] == [PASSED + K * i for i in range(3)]
+    OWN = col(rank, rank)
+    TILE = OWN - PAD if leads(rank) else OWN
+    X0 = 4 * (OWN - TILE)
+    pair = (rank, mate) if leads(rank) else (mate, rank)
+    assert all(col(s, pair[1]) == col(s, pair[0]) + K for s in faraway)
 
     eoff = topo.engines(core, cores[faraway[0]])
     eall = topo.engines(core, cores[mate])
     eon = [e for e in eall if e not in eoff]
     moff = topo.mask(core, cores[faraway[0]])
     mon = sum(1 << e for e in eon)
-    mall = topo.mask(core, cores[mate])
 
     sy, sl = g.sync, g.scalar
     sy.dma_start(T.lo[0:K, :], T.pl[:, :]).then_inc(S.lp, 16)
-    sy.dma_start(T.lo[K:SLOT, :], T.pl[0:16, 0:2]).then_inc(S.lp, 16)
-    sl.dma_start(T.xt[:, 0:4 * K], T.x[:, :]).then_inc(S.sx, 16)
+    sl.dma_start(T.lo[K:K + 36, :], T.pl[0:6, :]).then_inc(S.lp, 16)
+    sy.dma_start(T.xt[:, X0:X0 + 4 * K], T.x[:, :]).then_inc(S.sx, 16)
+    sl.dma_start(T.pk[G * (n - 1):G * n, 0:6], T.pl[:, :]).then_inc(S.ls, 16)
     sl.dma_start(T.bt[:, :], T.b[:, :]).then_inc(S.sb, 16)
     sy.dma_start(T.wt[:, :], T.w[:, :]).then_inc(S.sw, 16)
-    sy.dma_start(T.pk[G * (n - 1):G * n, 0:6], T.pl[:, :]).then_inc(S.ls, 16)
 
     g.iota(T.diag[:, :], [[-1, G]], 128, 1).then_inc(S.gi, 1)
     others = [s for s in order(rank)[:-1] if s != mate]
@@ -93,7 +98,7 @@ def rank_program(g, core, T, topo):
 
     g.remote_dma_fused([
         RemoteDMATransfer(dst_ids=[dst(s) for s in to], dma_engine_mask=1 << e, remote_sem=S.al,
-                          srcs=[T.lo[:, :]], dsts=[slot_at(s) for s in to])
+                          srcs=[T.lo[0:SLOT, :]], dsts=[slot_at(s) for s in to])
         for e, to in ((eoff[0], others[:half]), (eoff[len(eoff) // 2], others[half:] + [mate]))], local_sem=S.loc)
     loc = 2
     n_lists = n - 1
@@ -104,27 +109,26 @@ def rank_program(g, core, T, topo):
     def scales(a, m):
         return T.qs[:, a:a + m]
 
-    def to_far(view, sem):
-        return RemoteDMATransfer(dst_ids=[dst(s) for s in faraway], dma_engine_mask=moff, remote_sem=sem,
-                                 srcs=[view(OWN, K)], dsts=[view(col(s, rank), K) for s in faraway])
-
-    def to_mate(view, sem):
-        return RemoteDMATransfer(dst_ids=[dst(mate)], dma_engine_mask=mon, remote_sem=sem,
-                                 srcs=[view(OWN, K)], dsts=[view(MATE, K)])
+    def send(view, a, m, to, mask, sem):
+        g.remote_dma_fused([RemoteDMATransfer(dst_ids=[dst(s) for s, _ in to], dma_engine_mask=mask, remote_sem=sem,
+                                              srcs=[view(a, m)], dsts=[view(c, m) for _, c in to])], local_sem=S.loc)
 
     g.wait_ge(S.qx, 1)
-    g.remote_dma_fused([to_far(codes, S.ac)], local_sem=S.loc)
-    g.remote_dma_fused([to_mate(codes, S.pc)], local_sem=S.loc)
-    g.wait_ge(S.li, 1)
-    g.remote_dma_fused([to_far(scales, S.asc), to_mate(scales, S.psc)], local_sem=S.loc)
-    loc += 2 * (len(eoff) + len(eon))
-    n_far, n_mate = len(faraway) * len(eoff), len(eon)
-    rid, pid, _ = topo.addr(cores[mate])
-    g.wait_ge(S.ac, n_far)
-    g.remote_dma(codes(PASSED, 3 * K), codes(FAR, 3 * K), S.fc, S.loc, pid, rid, mon)
-    g.wait_ge(S.asc, n_far)
-    g.remote_dma(scales(PASSED, 3 * K), scales(FAR, 3 * K), S.fs, S.loc, pid, rid, mall)
-    loc += len(eon) + len(eall)
+    n_off, n_on = len(eoff), len(eon)
+    n_psc = n_on * len({beside(rank), col(rank, mate)})
+    for i, s in enumerate(faraway):
+        send(codes, OWN, K, [(s, col(s, rank))], moff, S["ac%d" % i])
+        if i == 0:
+            send(scales, OWN, K, [(mate, c) for c in sorted({beside(mate), col(mate, rank)})], mon, S.psc)
+            g.wait_ge(S.li, 1)
+    g.wait_ge(S.psc, n_psc)
+    send(scales, min(OWN, beside(rank)), 2 * K, [(s, col(s, pair[0])) for s in faraway], moff, S.asc)
+    send(codes, OWN, K, [(mate, col(mate, rank))], mon, S.pc)
+    for i in range(len(faraway)):
+        s = [s for s in faraway if far(s)[i] == rank][0]
+        g.wait_ge(S["ac%d" % i], n_off)
+        send(codes, col(rank, s), K, [(mate, col(mate, s))], mon, S.fc)
+    loc += 4 * n_off + 5 * n_on
     g.wait_ge(S.loc, loc)
 
     places = T.win[:, SLOT:SLOT * (B + 1):SLOT]
@@ -141,22 +145,21 @@ def rank_program(g, core, T, topo):
     def settle():
         ve.wait_ge(S.v, cnt[0])
 
-    did(ve.memset(T.xt[:, 4 * K:512], 0.0))
+    did(ve.memset(T.xt[:, 0:X0] if X0 else T.xt[:, 4 * K:512], 0.0))
     did(ve.memset(T.ones[:, :], 1.0))
     did(ve.memset(T.run[:, B:512], 0.0))
     settle()
     did(ve.tensor_tensor_scan(places, T.ones[:, :], T.ones[:, :], -1.0, ADD, MUL))
     ve.wait_ge(S.sx, 16)
-    ve.quantize_mx(T.qc[:, OWN:OWN + 128], T.qs[:, OWN:OWN + 128], T.xt[:, :]).then_inc(S.qx, 1)
+    ve.quantize_mx(T.qc[:, TILE:TILE + 128], T.qs[:, TILE:TILE + 128], T.xt[:, :]).then_inc(S.qx, 1)
     ve.wait_ge(S.gi, 1)
     did(ve.tensor_scalar(T.dm[:, :], T.diag[:, :], G - 1, None, AND))
-    did(ve.tensor_scalar(T.blk[:, :], T.diag[:, 0:1], 5, 3, SHR, AND))
-    did(ve.tensor_scalar(T.odd[:, :], T.diag[:, 0:1], G, None, AND))
+    did(ve.tensor_scalar(T.grp[:, :], T.diag[:, 0:1], 4, n - 1, SHR, AND))
+    did(ve.tensor_scalar(T.ch[:, :], T.diag[:, 0:1], 128.0 + G * (n - 1), float(OWN - B - K * (n - 1)), GE, MUL))
     settle()
-    did(ve.tensor_scalar(T.e0[:, :], T.dm[:, :], 0.0, float(DROP), EQ, MUL))
-    did(ve.tensor_scalar(T.e1[:, :], T.dm[:, :], G - 1.0, float(KEEP), EQ, MUL))
-    did(ve.tensor_scalar(T.cb[:, :], T.blk[:, :], 2.0 * PRIO + K, float(PRIO + B), MUL, ADD))
-    did(ve.tensor_scalar(T.ch[:, :], T.odd[:, :], (PRIO + 4.0 * K) / G, None, MUL))
+    did(ve.tensor_scalar(T.e0[:, :], T.dm[:, :], 0.0, DROP, EQ, MUL))
+    did(ve.tensor_scalar(T.e1[:, :], T.dm[:, :], G - 1.0, KEEP, EQ, MUL))
+    did(ve.tensor_scalar(T.cb[:, :], T.grp[:, :], float(K), float(B), MUL, ADD))
     did(ve.tensor_scalar(T.na[:, :], T.dm[:, 0:1], -1.0 / SLOT, -1.0 / SLOT, MUL, ADD))
     settle()
     ve.tensor_tensor(T.gate[:, 0:G], T.e0[:, :], T.e1[:, :], ADD).then_inc(S.g16, 1)
@@ -199,25 +202,23 @@ def rank_program(g, core, T, topo):
         did(ve.tensor_tensor(T.best[32 * h:32 * h + 32, :], T.t4[0:32, 0:20], T.t4[0:32, 20:40], MAX))
     settle()
     for h in (0, 1):
-        did(ve.tensor_scalar(T.bcol[64 * h:64 * h + 64, :], T.best[0:64, :], PRIO - 1, None, AND))
-    settle()
-    ve.tensor_copy(T.pick[:, :], T.bcol[:, :]).then_inc(S.of, 1)
-    ve.wait_ge(S.of, 1)
+        ve.tensor_scalar(T.pick[64 * h:64 * h + 64, :], T.best[0:64, :], -KEEP, T.e1[0:64, 0:1], ADD, ADD).then_inc(S.of, 1)
+    ve.wait_ge(S.of, 2)
     ve.wait_ge(S.qx, 1)
     ve.wait_ge(S.qb, 1)
-    ve.wait_ge(S.pc, n_mate)
-    ve.wait_ge(S.ac, n_far)
-    ve.wait_ge(S.fc, len(eon))
+    ve.wait_ge(S.pc, n_on)
+    for i in range(len(faraway)):
+        ve.wait_ge(S["ac%d" % i], n_off)
+    ve.wait_ge(S.fc, len(faraway) * n_on)
     for h, sem in ((0, S.pa), (1, S.pb)):
         ve.tensor_copy(T.mq[:, HALF * h:HALF * h + HALF].bitcast(dt.uint32),
                        T.qc[:, 0:WIDE].bitcast(dt.uint32).indirect(T.pick[:, 10 * h:10 * h + 10])).then_inc(sem, 1)
 
     sl.wait_ge(S.qx, 1)
     sl.wait_ge(S.qb, 1)
-    sl.wait_ge(S.of, 1)
-    sl.wait_ge(S.psc, n_mate)
-    sl.wait_ge(S.asc, n_far)
-    sl.wait_ge(S.fs, len(eall))
+    sl.wait_ge(S.of, 2)
+    sl.wait_ge(S.psc, n_psc)
+    sl.wait_ge(S.asc, len(faraway) * n_off)
     for h, sem in ((0, S.sa), (1, S.sb2)):
         sl.activation(T.ms[:, HALF * h:HALF * h + HALF], T.qs[:, 0:WIDE].indirect(T.pick[:, 10 * h:10 * h + 10]), COPY).then_inc(sem, 1)
 

@@ -6,8 +6,10 @@ G = 16
 PAD = 128 - K
 WIDE = B + 8 * K + PAD
 SLOT = 128
-HALF = B // 2
-KEEP, DROP = 2048.0, -8192.0
+CUT = (0, 160, B)
+KEEP = 2048.0
+STEP = 2 * KEEP
+DROP = -2 * G * STEP
 
 
 def _sb(n, t):
@@ -21,13 +23,13 @@ SCRATCH = {
     "qc": _sb(WIDE, C), "qs": _sb(WIDE + K, "uint8"), "wq": _sb(128 * O, C), "ws": _sb(128 * O, "uint8"),
     "mq": _sb(B, C), "ms": _sb(B, "uint8"),
     "ones": _sb(B, H), "diag": _sb(G, I), "dm": _sb(G, I), "grp": _sb(1, I), "cb": _sb(1, F), "ch": _sb(1, F),
-    "na": _sb(1, F), "e0": _sb(G, F), "e1": _sb(G, F), "gate": _sb(B, F), "val": _sb(K, F), "dump": _sb(6, F),
-    "pk": _sb(8, I), "zl": _sb(6, F), "off": _sb(6, U), "win": _sb(SLOT * (B + 1), F), "run": _sb(512, F),
-    "t1": _sb(32, F), "t2": _sb(32, F), "t3": _sb(64, F), "t4": _sb(40, F),
-    "best": _sb(20, F), "pick": _sb(20, U), "yt": _sb(O * B, F), "ps": ("psum", [128, 512 * 6], F),
+    "na": _sb(1, F), "lift": _sb(1, F), "fix": _sb(1, F), "e0": _sb(G, F), "e1": _sb(G, F), "gate": _sb(B, F),
+    "val": _sb(K, F), "dump": _sb(6, F),
+    "pk": _sb(6, I), "zl": _sb(6, F), "off": _sb(6, U), "win": _sb(SLOT * (B + 1), F), "run": _sb(512, F),
+    "t1": _sb(128, F), "t2": _sb(128, F), "best": _sb(32, F), "pick": _sb(20, U), "yt": _sb(O * B, F), "ps": ("psum", [128, 512 * 6], F),
 }
-SEMAPHORES = ["lp", "sx", "sb", "sw", "gi", "v", "a", "g16", "qx", "qb", "qw", "loc", "al", "ac0", "ac1", "ac2", "asc", "pc",
-              "psc", "fc", "ls", "li", "of", "pa", "pb", "sa", "sb2", "m0", "m1", "m2", "m3", "m4", "m5",
+SEMAPHORES = ["lp", "sx", "sb", "sw", "gi", "v", "a", "g16", "qx", "qb", "qw", "loc", "al", "ac0", "ac1", "ac2", "asc",
+              "psc", "cs", "fc", "ls", "li", "of", "pa", "pb", "sa", "sb2", "m0", "m1", "m2", "m3", "m4", "m5",
               "y0", "y1", "y2", "st"]
 
 
@@ -38,7 +40,7 @@ def rank_program(g, core, T, topo):
     cores, S = T.cores, T.sem
     n = len(cores)
     ADD, MUL, MAX, AND = AluOpType.add, AluOpType.mult, AluOpType.max, AluOpType.bitwise_and
-    SHR, EQ, GE = AluOpType.arith_shift_right, AluOpType.is_equal, AluOpType.is_ge
+    SHR, EQ, GE, SUB = AluOpType.arith_shift_right, AluOpType.is_equal, AluOpType.is_ge, AluOpType.subtract
     COPY = ActivationFunctionType.Copy
 
     def order(r):
@@ -84,22 +86,22 @@ def rank_program(g, core, T, topo):
     sy.dma_start(T.lo[0:K, :], T.pl[:, :]).then_inc(S.lp, 16)
     sl.dma_start(T.lo[K:K + 36, :], T.pl[0:6, :]).then_inc(S.lp, 16)
     sy.dma_start(T.xt[:, X0:X0 + 4 * K], T.x[:, :]).then_inc(S.sx, 16)
-    sl.dma_start(T.pk[G * (n - 1):G * n, 0:6], T.pl[:, :]).then_inc(S.ls, 16)
+    sl.dma_start(T.pk[G * (n - 1):G * n, :], T.pl[:, :]).then_inc(S.ls, 16)
     sl.dma_start(T.bt[:, :], T.b[:, :]).then_inc(S.sb, 16)
     sy.dma_start(T.wt[:, :], T.w[:, :]).then_inc(S.sw, 16)
 
     g.iota(T.diag[:, :], [[-1, G]], 128, 1).then_inc(S.gi, 1)
-    others = [s for s in order(rank)[:-1] if s != mate]
-    half = len(others) // 2
-    g.wait_ge(S.lp, 32)
+    slots = [(s, order(s).index(rank)) for s in order(rank)[:-1]]
+    slots.sort(key=lambda st: st[0] == mate)
+    halves = (slots[0::2], slots[1::2])
 
-    def slot_at(r):
-        return T.land[order(r).index(rank)]
+    def lists():
+        g.wait_ge(S.lp, 32)
+        g.remote_dma_fused([
+            RemoteDMATransfer(dst_ids=[dst(s) for s, _ in to], dma_engine_mask=1 << e, remote_sem=S.al,
+                              srcs=[T.lo[0:SLOT, :]], dsts=[T.land[t] for _, t in to])
+            for e, to in zip((eoff[0], eoff[len(eoff) // 2]), halves)], local_sem=S.loc)
 
-    g.remote_dma_fused([
-        RemoteDMATransfer(dst_ids=[dst(s) for s in to], dma_engine_mask=1 << e, remote_sem=S.al,
-                          srcs=[T.lo[0:SLOT, :]], dsts=[slot_at(s) for s in to])
-        for e, to in ((eoff[0], others[:half]), (eoff[len(eoff) // 2], others[half:] + [mate]))], local_sem=S.loc)
     loc = 2
     n_lists = n - 1
 
@@ -109,31 +111,47 @@ def rank_program(g, core, T, topo):
     def scales(a, m):
         return T.qs[:, a:a + m]
 
-    def send(view, a, m, to, mask, sem):
-        g.remote_dma_fused([RemoteDMATransfer(dst_ids=[dst(s) for s, _ in to], dma_engine_mask=mask, remote_sem=sem,
-                                              srcs=[view(a, m)], dsts=[view(c, m) for _, c in to])], local_sem=S.loc)
+    def move(view, a, m, to, mask, sem):
+        return RemoteDMATransfer(dst_ids=[dst(s) for s, _ in to], dma_engine_mask=mask, remote_sem=sem,
+                                 srcs=[view(a, m)], dsts=[view(c, m) for _, c in to])
 
-    g.wait_ge(S.qx, 1)
-    n_off, n_on = len(eoff), len(eon)
-    n_psc = n_on * len({beside(rank), col(rank, mate)})
-    for i, s in enumerate(faraway):
-        send(codes, OWN, K, [(s, col(s, rank))], moff, S["ac%d" % i])
-        if i == 0:
-            send(scales, OWN, K, [(mate, c) for c in sorted({beside(mate), col(mate, rank)})], mon, S.psc)
-            g.wait_ge(S.li, 1)
-    g.wait_ge(S.psc, n_psc)
-    send(scales, min(OWN, beside(rank)), 2 * K, [(s, col(s, pair[0])) for s in faraway], moff, S.asc)
-    send(codes, OWN, K, [(mate, col(mate, rank))], mon, S.pc)
-    for i in range(len(faraway)):
+    def call(*moves):
+        g.remote_dma_fused(list(moves), local_sem=S.loc)
+
+    def out(i):
+        return move(codes, OWN, K, [(faraway[i], col(faraway[i], rank))], moff, S["ac%d" % i])
+
+    def hand_on(i):
         s = [s for s in faraway if far(s)[i] == rank][0]
         g.wait_ge(S["ac%d" % i], n_off)
-        send(codes, col(rank, s), K, [(mate, col(mate, s))], mon, S.fc)
+        return move(codes, col(rank, s), K, [(mate, col(mate, s))], mon, S.fc)
+
+    n_off, n_on = len(eoff), len(eon)
+    n_psc = n_on
+    lists()
+    g.wait_ge(S.qx, 1)
+    call(out(0))
+    call(move(scales, OWN, K, [(mate, beside(mate))], mon, S.psc))
+    g.wait_ge(S.li, 1)
+    call(out(1), move(codes, OWN, K, [(mate, col(mate, rank))], mon, S.fc))
+    call(out(2))
+    g.wait_ge(S.psc, n_psc)
+    call(move(scales, min(OWN, beside(rank)), 2 * K, [(s, col(s, pair[0])) for s in faraway], moff, S.asc))
+    for i in range(len(faraway)):
+        call(hand_on(i))
     loc += 4 * n_off + 5 * n_on
     g.wait_ge(S.loc, loc)
 
     places = T.win[:, SLOT:SLOT * (B + 1):SLOT]
+    sl.wait_ge(S.g16, 1)
+    have, steps = G, 0
+    while have < B:
+        m = min(have, B - have)
+        sl.activation(T.gate[:, have:have + m], T.gate[:, 0:m], COPY).then_inc(S.a, 1)
+        have, steps = have + m, steps + 1
+        sl.wait_ge(S.a, steps)
     sy.wait_ge(S.al, n_lists)
-    sy.dma_start(T.pk[0:G * n_lists, 0:6], T.land[0:n_lists, 0:K, :]).then_inc(S.ls, 16)
+    sy.dma_start(T.pk[0:G * n_lists, :], T.land[:, 0:K, :]).then_inc(S.ls, 16)
     sy.sem_inc(S.li, 1)
 
     ve, cnt = g.vector, [0]
@@ -148,38 +166,36 @@ def rank_program(g, core, T, topo):
     did(ve.memset(T.xt[:, 0:X0] if X0 else T.xt[:, 4 * K:512], 0.0))
     did(ve.memset(T.ones[:, :], 1.0))
     did(ve.memset(T.run[:, B:512], 0.0))
-    settle()
-    did(ve.tensor_tensor_scan(places, T.ones[:, :], T.ones[:, :], -1.0, ADD, MUL))
-    ve.wait_ge(S.sx, 16)
-    ve.quantize_mx(T.qc[:, TILE:TILE + 128], T.qs[:, TILE:TILE + 128], T.xt[:, :]).then_inc(S.qx, 1)
     ve.wait_ge(S.gi, 1)
     did(ve.tensor_scalar(T.dm[:, :], T.diag[:, :], G - 1, None, AND))
-    did(ve.tensor_scalar(T.grp[:, :], T.diag[:, 0:1], 4, n - 1, SHR, AND))
-    did(ve.tensor_scalar(T.ch[:, :], T.diag[:, 0:1], 128.0 + G * (n - 1), float(OWN - B - K * (n - 1)), GE, MUL))
     settle()
     did(ve.tensor_scalar(T.e0[:, :], T.dm[:, :], 0.0, DROP, EQ, MUL))
     did(ve.tensor_scalar(T.e1[:, :], T.dm[:, :], G - 1.0, KEEP, EQ, MUL))
-    did(ve.tensor_scalar(T.cb[:, :], T.grp[:, :], float(K), float(B), MUL, ADD))
-    did(ve.tensor_scalar(T.na[:, :], T.dm[:, 0:1], -1.0 / SLOT, -1.0 / SLOT, MUL, ADD))
+    did(ve.tensor_scalar(T.lift[:, :], T.dm[:, 0:1], STEP, -1.0, MUL, ADD))
     settle()
     ve.tensor_tensor(T.gate[:, 0:G], T.e0[:, :], T.e1[:, :], ADD).then_inc(S.g16, 1)
+    did(ve.tensor_tensor_scan(places, T.ones[:, :], T.ones[:, :], T.lift[:, :], ADD, MUL))
+    ve.wait_ge(S.sx, 16)
+    ve.quantize_mx(T.qc[:, TILE:TILE + 128], T.qs[:, TILE:TILE + 128], T.xt[:, :]).then_inc(S.qx, 1)
+    did(ve.tensor_scalar(T.grp[:, :], T.diag[:, 0:1], 4, n - 1, SHR, AND))
+    did(ve.tensor_scalar(T.ch[:, :], T.diag[:, 0:1], 128.0 + G * (n - 1), float(OWN - B - K * (n - 1)), GE, MUL))
+    did(ve.tensor_scalar(T.na[:, :], T.dm[:, 0:1], (STEP - 1.0) / SLOT, -1.0 / SLOT, MUL, ADD))
+    did(ve.tensor_scalar(T.fix[:, :], T.e1[:, 0:1], T.lift[:, :], -KEEP - 1.0, SUB, ADD))
+    settle()
+    did(ve.tensor_scalar(T.cb[:, :], T.grp[:, :], float(K), float(B), MUL, ADD))
+    settle()
     did(ve.tensor_scalar(T.val[:, :], T.win[:, SLOT:SLOT * (K + 1):SLOT], T.cb[:, :], T.ch[:, :], ADD, ADD))
     did(ve.tensor_scalar(T.dump[:, :], T.win[:, SLOT:SLOT * (K + 1):SLOT * G], -1.0 / SLOT, T.na[:, :], MUL, ADD))
     ve.wait_ge(S.sb, 16)
     ve.quantize_mx(T.qc[:, 0:B], T.qs[:, 0:B], T.bt[:, :]).then_inc(S.qb, 1)
     ve.wait_ge(S.sw, 16)
     ve.quantize_mx(T.wq[:, :], T.ws[:, :], T.wt[:, :]).then_inc(S.qw, 1)
-    sl.wait_ge(S.g16, 1)
-    have, steps = G, 0
-    while have < B:
-        m = min(have, B - have)
-        sl.activation(T.gate[:, have:have + m], T.gate[:, 0:m], COPY).then_inc(S.a, 1)
-        have, steps = have + m, steps + 1
-        sl.wait_ge(S.a, steps)
     settle()
     ve.wait_ge(S.a, steps)
+    ve.wait_ge(S.qx, 1)
+    ve.wait_ge(S.qb, 1)
     ve.wait_ge(S.ls, 32)
-    did(ve.tensor_tensor(T.zl[:, :], T.pk[:, 0:6], T.dump[:, :], MAX))
+    did(ve.tensor_tensor(T.zl[:, :], T.pk[:, :], T.dump[:, :], MAX))
     settle()
     did(ve.tensor_scalar(T.off[:, :], T.zl[:, :], float(SLOT), float(SLOT), MUL, ADD))
     settle()
@@ -187,62 +203,62 @@ def rank_program(g, core, T, topo):
     settle()
     did(ve.tensor_tensor_scan(T.run[:, 0:B], T.gate[:, :], places, 0.0, ADD, MAX))
     settle()
-    did(ve.transpose(T.t1[:, :], T.run[:, G - 1:512:G]))
+    for k in range(4):
+        did(ve.transpose(T.t1[0:32, k:128:4], T.run[32 * k:32 * k + 32, G - 1:512:G]))
     settle()
     for h in (0, 1):
-        did(ve.tensor_tensor(T.t2[:, G * h:G * h + G], T.t1[:, 0:G], T.t1[:, G:2 * G], MAX))
+        did(ve.tensor_tensor_scan(T.t2[0:32, 64 * h:64 * h + 64], T.t1[0:32, 0:64], T.t1[0:32, 64:128], 0.0, MAX, MAX))
     settle()
     for h in (0, 1):
-        did(ve.transpose(T.t3[0:64, 32 * h:32 * h + 32], T.t2[64 * h:64 * h + 64, :]))
+        did(ve.transpose(T.best[32 * h:32 * h + 32, :], T.t2[0:32, 3:128:4]))
     settle()
     for h in (0, 1):
-        did(ve.tensor_tensor(T.t4[0:32, 20 * h:20 * h + 20], T.t3[32 * h:32 * h + 32, 0:20], T.t3[32 * h:32 * h + 32, 32:52], MAX))
-    settle()
-    for h in (0, 1):
-        did(ve.tensor_tensor(T.best[32 * h:32 * h + 32, :], T.t4[0:32, 0:20], T.t4[0:32, 20:40], MAX))
-    settle()
-    for h in (0, 1):
-        ve.tensor_scalar(T.pick[64 * h:64 * h + 64, :], T.best[0:64, :], -KEEP, T.e1[0:64, 0:1], ADD, ADD).then_inc(S.of, 1)
-    ve.wait_ge(S.of, 2)
-    ve.wait_ge(S.qx, 1)
-    ve.wait_ge(S.qb, 1)
-    ve.wait_ge(S.pc, n_on)
+        ve.tensor_scalar(T.pick[64 * h:64 * h + 64, :], T.best[0:64, 0:20], T.fix[0:64, :], None, ADD).then_inc(S.of, 1)
     for i in range(len(faraway)):
         ve.wait_ge(S["ac%d" % i], n_off)
-    ve.wait_ge(S.fc, len(faraway) * n_on)
+    ve.wait_ge(S.fc, (len(faraway) + 1) * n_on)
+    ve.wait_ge(S.of, 2)
     for h, sem in ((0, S.pa), (1, S.pb)):
-        ve.tensor_copy(T.mq[:, HALF * h:HALF * h + HALF].bitcast(dt.uint32),
-                       T.qc[:, 0:WIDE].bitcast(dt.uint32).indirect(T.pick[:, 10 * h:10 * h + 10])).then_inc(sem, 1)
+        ve.tensor_copy(T.mq[:, CUT[h]:CUT[h + 1]].bitcast(dt.uint32),
+                       T.qc[:, 0:WIDE].bitcast(dt.uint32).indirect(T.pick[:, CUT[h] // G:CUT[h + 1] // G])).then_inc(sem, 1)
 
     sl.wait_ge(S.qx, 1)
     sl.wait_ge(S.qb, 1)
-    sl.wait_ge(S.of, 2)
     sl.wait_ge(S.psc, n_psc)
+    if leads(rank):
+        sl.wait_ge(S.li, 1)
+        sl.dma_start(scales(col(rank, mate), K), scales(beside(rank), K)).then_inc(S.cs, 16)
+        sl.wait_ge(S.cs, 16)
     sl.wait_ge(S.asc, len(faraway) * n_off)
+    sl.wait_ge(S.of, 2)
     for h, sem in ((0, S.sa), (1, S.sb2)):
-        sl.activation(T.ms[:, HALF * h:HALF * h + HALF], T.qs[:, 0:WIDE].indirect(T.pick[:, 10 * h:10 * h + 10]), COPY).then_inc(sem, 1)
+        sl.activation(T.ms[:, CUT[h]:CUT[h + 1]], T.qs[:, 0:WIDE].indirect(T.pick[:, CUT[h] // G:CUT[h + 1] // G]),
+                      COPY).then_inc(sem, 1)
 
     te = g.tensor
-    runs = [(0, 0), (1, 0), (0, 1), (1, 1), (2, 0), (2, 1)]
+    runs = [(0, 0), (2, 0), (1, 0), (0, 1), (1, 1), (2, 1)]
     te.wait_ge(S.qw, 1)
-    waited = []
     for i, (r, h) in enumerate(runs):
-        if h not in waited:
+        if r == 0:
             te.wait_ge((S.pa, S.pb)[h], 1)
             te.wait_ge((S.sa, S.sb2)[h], 1)
-            waited.append(h)
-        te.matmul_mx(T.ps[:, 512 * i:512 * i + HALF], T.wq[:, 128 * r:128 * r + 128], T.ws[:, 128 * r:128 * r + 128],
-                     T.mq[:, HALF * h:HALF * h + HALF], T.ms[:, HALF * h:HALF * h + HALF], True, True).then_inc(S["m%d" % i], 1)
+        a, b = CUT[h], CUT[h + 1]
+        te.matmul_mx(T.ps[:, 512 * i:512 * i + b - a], T.wq[:, 128 * r:128 * r + 128], T.ws[:, 128 * r:128 * r + 128],
+                     T.mq[:, a:b], T.ms[:, a:b], True, True).then_inc(S["m%d" % i], 1)
+    stores = [(0, 1), (1, 3), (3, 6)]
     for i, (r, h) in enumerate(runs):
-        out = T.yt[:, B * r + HALF * h:B * r + HALF * h + HALF]
-        src = T.ps[:, 512 * i:512 * i + HALF]
-        if (r, h) in ((0, 0), (0, 1), (2, 1)):
+        out = T.yt[:, B * r + CUT[h]:B * r + CUT[h + 1]]
+        src = T.ps[:, 512 * i:512 * i + CUT[h + 1] - CUT[h]]
+        done = S["y%d" % [k for k, (a, b) in enumerate(stores) if a <= 2 * r + h < b][0]]
+        if i % 2 == 0:
             ve.wait_ge(S["m%d" % i], 1)
-            ve.tensor_copy(out, src).then_inc(S["y%d" % r], 1)
+            ve.tensor_copy(out, src).then_inc(done, 1)
         else:
             sl.wait_ge(S["m%d" % i], 1)
-            sl.activation(out, src, COPY).then_inc(S["y%d" % r], 1)
-    for r in range(O):
-        sy.wait_ge(S["y%d" % r], 2)
-        sy.dma_start(T.y[:, B * r:B * r + B], T.yt[:, B * r:B * r + B]).then_inc(S.st, 16)
-    sy.wait_ge(S.st, 48)
+            sl.activation(out, src, COPY).then_inc(done, 1)
+    for k, (a, b) in enumerate(stores):
+        q = sl if b == len(runs) else sy
+        q.wait_ge(S["y%d" % k], b - a)
+        c, d = (B * (j // 2) + CUT[j % 2] for j in (a, b))
+        q.dma_start(T.y[:, c:d], T.yt[:, c:d]).then_inc(S.st, 16)
+    sy.wait_ge(S.st, 16 * len(stores))

from concourse.bass import DstId, RemoteDMATransfer
from concourse.mybir import dt, AluOpType, ActivationFunctionType

B, K, O = 320, 96, 3
G = 16
PAD = 128 - K
WIDE = B + 8 * K + PAD
SLOT = 128
CUT = (0, 160, B)
KEEP = 2048.0
STEP = 2 * KEEP
DROP = -2 * G * STEP


def _sb(n, t):
    return ("sbuf", [128, n], t)


F, I, U, H, C = "float32", "int32", "uint16", "bfloat16", "float8_e4m3fn_x4"
SCRATCH = {
    "lo": ("dram", [K + 36, 1], I), "land": ("dram", [7, SLOT, 1], I),
    "xt": _sb(512, H), "bt": _sb(4 * B, H), "wt": _sb(512 * O, H),
    "qc": _sb(WIDE, C), "qs": _sb(WIDE + K, "uint8"), "wq": _sb(128 * O, C), "ws": _sb(128 * O, "uint8"),
    "mq": _sb(B, C), "ms": _sb(B, "uint8"),
    "ones": _sb(B, H), "diag": _sb(G, I), "dm": _sb(G, I), "grp": _sb(1, I), "cb": _sb(1, F), "ch": _sb(1, F),
    "na": _sb(1, F), "lift": _sb(1, F), "fix": _sb(1, F), "e0": _sb(G, F), "e1": _sb(G, F), "gate": _sb(B, F),
    "val": _sb(K, F), "dump": _sb(6, F),
    "pk": _sb(6, I), "zl": _sb(6, F), "off": _sb(6, U), "win": _sb(SLOT * (B + 1), F), "run": _sb(512, F),
    "t1": _sb(128, F), "t2": _sb(128, F), "best": _sb(32, F), "pick": _sb(20, U), "yt": _sb(O * B, F), "ps": ("psum", [128, 512 * 6], F),
}
SEMAPHORES = ["lp", "sx", "sb", "sw", "gi", "v", "a", "g16", "qx", "qb", "qw", "loc", "al", "ac0", "ac1", "ac2", "asc",
              "psc", "cs", "fc", "ls", "li", "of", "pa", "pb", "sa", "sb2", "m0", "m1", "m2", "m3", "m4", "m5",
              "y0", "y1", "y2", "st"]


def rank_program(g, core, T, topo):
    rank = T.rank_of(core)
    if rank is None:
        return
    cores, S = T.cores, T.sem
    n = len(cores)
    ADD, MUL, MAX, AND = AluOpType.add, AluOpType.mult, AluOpType.max, AluOpType.bitwise_and
    SHR, EQ, GE, SUB = AluOpType.arith_shift_right, AluOpType.is_equal, AluOpType.is_ge, AluOpType.subtract
    COPY = ActivationFunctionType.Copy

    def order(r):
        return [(r + 1 + i) % n for i in range(n)]

    def same_chip(a, b):
        return topo.chip(cores[a]) == topo.chip(cores[b])

    def far(r):
        return [s for s in order(r)[:-1] if not same_chip(r, s) and topo.die(cores[s]) == topo.die(cores[r])]

    def partner(r):
        return [s for s in order(r)[:-1] if same_chip(r, s)][0]

    def dst(r):
        rid, pid, _ = topo.addr(cores[r])
        return DstId(rid=rid, pnc=pid)

    def leads(r):
        return order(r)[0] == partner(r)

    def col(r, s):
        return B + K * order(r).index(s) + (PAD if s == r and leads(r) else 0)

    def beside(r):
        return col(r, r) + K if leads(r) else col(r, partner(r))

    mate = partner(rank)
    faraway = far(rank)
    OWN = col(rank, rank)
    TILE = OWN - PAD if leads(rank) else OWN
    X0 = 4 * (OWN - TILE)
    pair = (rank, mate) if leads(rank) else (mate, rank)
    assert all(col(s, pair[1]) == col(s, pair[0]) + K for s in faraway)

    eoff = topo.engines(core, cores[faraway[0]])
    eall = topo.engines(core, cores[mate])
    eon = [e for e in eall if e not in eoff]
    moff = topo.mask(core, cores[faraway[0]])
    mon = sum(1 << e for e in eon)

    sy, sl = g.sync, g.scalar
    sy.dma_start(T.lo[0:K, :], T.pl[:, :]).then_inc(S.lp, 16)
    sl.dma_start(T.lo[K:K + 36, :], T.pl[0:6, :]).then_inc(S.lp, 16)
    sy.dma_start(T.xt[:, X0:X0 + 4 * K], T.x[:, :]).then_inc(S.sx, 16)
    sl.dma_start(T.pk[G * (n - 1):G * n, :], T.pl[:, :]).then_inc(S.ls, 16)
    sl.dma_start(T.bt[:, :], T.b[:, :]).then_inc(S.sb, 16)
    sy.dma_start(T.wt[:, :], T.w[:, :]).then_inc(S.sw, 16)

    g.iota(T.diag[:, :], [[-1, G]], 128, 1).then_inc(S.gi, 1)
    slots = [(s, order(s).index(rank)) for s in order(rank)[:-1]]
    slots.sort(key=lambda st: st[0] == mate)
    halves = (slots[0::2], slots[1::2])

    def lists():
        g.wait_ge(S.lp, 32)
        g.remote_dma_fused([
            RemoteDMATransfer(dst_ids=[dst(s) for s, _ in to], dma_engine_mask=1 << e, remote_sem=S.al,
                              srcs=[T.lo[0:SLOT, :]], dsts=[T.land[t] for _, t in to])
            for e, to in zip((eoff[0], eoff[len(eoff) // 2]), halves)], local_sem=S.loc)

    loc = 2
    n_lists = n - 1

    def codes(a, m):
        return T.qc[:, a:a + m].bitcast(dt.uint8)

    def scales(a, m):
        return T.qs[:, a:a + m]

    def move(view, a, m, to, mask, sem):
        return RemoteDMATransfer(dst_ids=[dst(s) for s, _ in to], dma_engine_mask=mask, remote_sem=sem,
                                 srcs=[view(a, m)], dsts=[view(c, m) for _, c in to])

    def call(*moves):
        g.remote_dma_fused(list(moves), local_sem=S.loc)

    def out(i):
        return move(codes, OWN, K, [(faraway[i], col(faraway[i], rank))], moff, S["ac%d" % i])

    def hand_on(i):
        s = [s for s in faraway if far(s)[i] == rank][0]
        g.wait_ge(S["ac%d" % i], n_off)
        return move(codes, col(rank, s), K, [(mate, col(mate, s))], mon, S.fc)

    n_off, n_on = len(eoff), len(eon)
    n_psc = n_on
    lists()
    g.wait_ge(S.qx, 1)
    call(out(0))
    call(move(scales, OWN, K, [(mate, beside(mate))], mon, S.psc))
    g.wait_ge(S.li, 1)
    call(out(1), move(codes, OWN, K, [(mate, col(mate, rank))], mon, S.fc))
    call(out(2))
    g.wait_ge(S.psc, n_psc)
    call(move(scales, min(OWN, beside(rank)), 2 * K, [(s, col(s, pair[0])) for s in faraway], moff, S.asc))
    for i in range(len(faraway)):
        call(hand_on(i))
    loc += 4 * n_off + 5 * n_on
    g.wait_ge(S.loc, loc)

    places = T.win[:, SLOT:SLOT * (B + 1):SLOT]
    sl.wait_ge(S.g16, 1)
    have, steps = G, 0
    while have < B:
        m = min(have, B - have)
        sl.activation(T.gate[:, have:have + m], T.gate[:, 0:m], COPY).then_inc(S.a, 1)
        have, steps = have + m, steps + 1
        sl.wait_ge(S.a, steps)
    sy.wait_ge(S.al, n_lists)
    sy.dma_start(T.pk[0:G * n_lists, :], T.land[:, 0:K, :]).then_inc(S.ls, 16)
    sy.sem_inc(S.li, 1)

    ve, cnt = g.vector, [0]

    def did(ins):
        ins.then_inc(S.v, 1)
        cnt[0] += 1

    def settle():
        ve.wait_ge(S.v, cnt[0])

    did(ve.memset(T.xt[:, 0:X0] if X0 else T.xt[:, 4 * K:512], 0.0))
    did(ve.memset(T.ones[:, :], 1.0))
    did(ve.memset(T.run[:, B:512], 0.0))
    ve.wait_ge(S.gi, 1)
    did(ve.tensor_scalar(T.dm[:, :], T.diag[:, :], G - 1, None, AND))
    settle()
    did(ve.tensor_scalar(T.e0[:, :], T.dm[:, :], 0.0, DROP, EQ, MUL))
    did(ve.tensor_scalar(T.e1[:, :], T.dm[:, :], G - 1.0, KEEP, EQ, MUL))
    did(ve.tensor_scalar(T.lift[:, :], T.dm[:, 0:1], STEP, -1.0, MUL, ADD))
    settle()
    ve.tensor_tensor(T.gate[:, 0:G], T.e0[:, :], T.e1[:, :], ADD).then_inc(S.g16, 1)
    did(ve.tensor_tensor_scan(places, T.ones[:, :], T.ones[:, :], T.lift[:, :], ADD, MUL))
    ve.wait_ge(S.sx, 16)
    ve.quantize_mx(T.qc[:, TILE:TILE + 128], T.qs[:, TILE:TILE + 128], T.xt[:, :]).then_inc(S.qx, 1)
    did(ve.tensor_scalar(T.grp[:, :], T.diag[:, 0:1], 4, n - 1, SHR, AND))
    did(ve.tensor_scalar(T.ch[:, :], T.diag[:, 0:1], 128.0 + G * (n - 1), float(OWN - B - K * (n - 1)), GE, MUL))
    did(ve.tensor_scalar(T.na[:, :], T.dm[:, 0:1], (STEP - 1.0) / SLOT, -1.0 / SLOT, MUL, ADD))
    did(ve.tensor_scalar(T.fix[:, :], T.e1[:, 0:1], T.lift[:, :], -KEEP - 1.0, SUB, ADD))
    settle()
    did(ve.tensor_scalar(T.cb[:, :], T.grp[:, :], float(K), float(B), MUL, ADD))
    settle()
    did(ve.tensor_scalar(T.val[:, :], T.win[:, SLOT:SLOT * (K + 1):SLOT], T.cb[:, :], T.ch[:, :], ADD, ADD))
    did(ve.tensor_scalar(T.dump[:, :], T.win[:, SLOT:SLOT * (K + 1):SLOT * G], -1.0 / SLOT, T.na[:, :], MUL, ADD))
    ve.wait_ge(S.sb, 16)
    ve.quantize_mx(T.qc[:, 0:B], T.qs[:, 0:B], T.bt[:, :]).then_inc(S.qb, 1)
    ve.wait_ge(S.sw, 16)
    ve.quantize_mx(T.wq[:, :], T.ws[:, :], T.wt[:, :]).then_inc(S.qw, 1)
    settle()
    ve.wait_ge(S.a, steps)
    ve.wait_ge(S.qx, 1)
    ve.wait_ge(S.qb, 1)
    ve.wait_ge(S.ls, 32)
    did(ve.tensor_tensor(T.zl[:, :], T.pk[:, :], T.dump[:, :], MAX))
    settle()
    did(ve.tensor_scalar(T.off[:, :], T.zl[:, :], float(SLOT), float(SLOT), MUL, ADD))
    settle()
    did(ve.tensor_copy(T.win[:, :].indirect(T.off[:, :]), T.val[:, :]))
    settle()
    did(ve.tensor_tensor_scan(T.run[:, 0:B], T.gate[:, :], places, 0.0, ADD, MAX))
    settle()
    for k in range(4):
        did(ve.transpose(T.t1[0:32, k:128:4], T.run[32 * k:32 * k + 32, G - 1:512:G]))
    settle()
    for h in (0, 1):
        did(ve.tensor_tensor_scan(T.t2[0:32, 64 * h:64 * h + 64], T.t1[0:32, 0:64], T.t1[0:32, 64:128], 0.0, MAX, MAX))
    settle()
    for h in (0, 1):
        did(ve.transpose(T.best[32 * h:32 * h + 32, :], T.t2[0:32, 3:128:4]))
    settle()
    for h in (0, 1):
        ve.tensor_scalar(T.pick[64 * h:64 * h + 64, :], T.best[0:64, 0:20], T.fix[0:64, :], None, ADD).then_inc(S.of, 1)
    for i in range(len(faraway)):
        ve.wait_ge(S["ac%d" % i], n_off)
    ve.wait_ge(S.fc, (len(faraway) + 1) * n_on)
    ve.wait_ge(S.of, 2)
    for h, sem in ((0, S.pa), (1, S.pb)):
        ve.tensor_copy(T.mq[:, CUT[h]:CUT[h + 1]].bitcast(dt.uint32),
                       T.qc[:, 0:WIDE].bitcast(dt.uint32).indirect(T.pick[:, CUT[h] // G:CUT[h + 1] // G])).then_inc(sem, 1)

    sl.wait_ge(S.qx, 1)
    sl.wait_ge(S.qb, 1)
    sl.wait_ge(S.psc, n_psc)
    if leads(rank):
        sl.wait_ge(S.li, 1)
        sl.dma_start(scales(col(rank, mate), K), scales(beside(rank), K)).then_inc(S.cs, 16)
        sl.wait_ge(S.cs, 16)
    sl.wait_ge(S.asc, len(faraway) * n_off)
    sl.wait_ge(S.of, 2)
    for h, sem in ((0, S.sa), (1, S.sb2)):
        sl.activation(T.ms[:, CUT[h]:CUT[h + 1]], T.qs[:, 0:WIDE].indirect(T.pick[:, CUT[h] // G:CUT[h + 1] // G]),
                      COPY).then_inc(sem, 1)

    te = g.tensor
    runs = [(0, 0), (2, 0), (1, 0), (0, 1), (1, 1), (2, 1)]
    te.wait_ge(S.qw, 1)
    for i, (r, h) in enumerate(runs):
        if r == 0:
            te.wait_ge((S.pa, S.pb)[h], 1)
            te.wait_ge((S.sa, S.sb2)[h], 1)
        a, b = CUT[h], CUT[h + 1]
        te.matmul_mx(T.ps[:, 512 * i:512 * i + b - a], T.wq[:, 128 * r:128 * r + 128], T.ws[:, 128 * r:128 * r + 128],
                     T.mq[:, a:b], T.ms[:, a:b], True, True).then_inc(S["m%d" % i], 1)
    stores = [(0, 1), (1, 3), (3, 6)]
    for i, (r, h) in enumerate(runs):
        out = T.yt[:, B * r + CUT[h]:B * r + CUT[h + 1]]
        src = T.ps[:, 512 * i:512 * i + CUT[h + 1] - CUT[h]]
        done = S["y%d" % [k for k, (a, b) in enumerate(stores) if a <= 2 * r + h < b][0]]
        if i % 2 == 0:
            ve.wait_ge(S["m%d" % i], 1)
            ve.tensor_copy(out, src).then_inc(done, 1)
        else:
            sl.wait_ge(S["m%d" % i], 1)
            sl.activation(out, src, COPY).then_inc(done, 1)
    for k, (a, b) in enumerate(stores):
        q = sl if b == len(runs) else sy
        q.wait_ge(S["y%d" % k], b - a)
        c, d = (B * (j // 2) + CUT[j % 2] for j in (a, b))
        q.dma_start(T.y[:, c:d], T.yt[:, c:d]).then_inc(S.st, 16)
    sy.wait_ge(S.st, 16 * len(stores))
